import numpy as np, ml_dtypes
CORES = [35,38,43,46]
N = 4
KB, QP = 2, 256
MEM = [0]
def setup_inputs(rng):
    return {"q": rng.standard_normal((N, 128, QP), dtype=np.float32).astype(ml_dtypes.bfloat16), "k": rng.standard_normal((N, 128, KB * 128), dtype=np.float32).astype(ml_dtypes.bfloat16), "v": rng.standard_normal((N, 128, KB * 128), dtype=np.float32).astype(ml_dtypes.bfloat16)}
def setup_inputs_big(rng):
    d = setup_inputs(rng)
    for k in ("q", "k", "v"): d[k] = (d[k].astype(np.float32) * 1024.0).astype(d[k].dtype)
    return d
def setup_inputs_small(rng):
    d = setup_inputs(rng)
    for k in ("q", "k", "v"): d[k] = (d[k].astype(np.float32) * (1 / 1024.0)).astype(d[k].dtype)
    return d
def setup_inputs_apart(rng):
    d = setup_inputs(rng)
    f = (10.0 ** rng.permutation(np.linspace(-1.5, 1.5, N))).astype(np.float32).reshape(N, 1, 1)
    for k in ("q", "k", "v"): d[k] = (d[k].astype(np.float32) * f).astype(d[k].dtype)
    return d
def reference(q, k, v):
    Q, K, V = q.astype(np.float64), k.astype(np.float64), v.astype(np.float64)
    y = np.zeros((N, 128, QP))
    for r in range(N):
        for j in MEM:
            for b in range(KB):
                S = np.maximum(K[j][:, 128 * b:128 * b + 128].T @ Q[r], 0.0)
                y[r] += V[j][:, 128 * b:128 * b + 128].T @ S
    return {"y": y.astype(ml_dtypes.bfloat16 if q.dtype != np.float64 else np.float64)}

@@ -1,0 +1,107 @@
+from concourse.bass import DstId, RemoteDMATransfer
+from concourse.mybir import AluOpType
+
+P = 128
+QP = 256
+KB = 2
+W = KB * P
+
+SCRATCH = {
+    "kv": ("sbuf", [P, 2 * W], "bfloat16"),
+    "qs": ("sbuf", [P, QP], "bfloat16"),
+    "zero": ("sbuf", [P, QP], "float32"),
+    "s0": ("sbuf", [P, QP], "bfloat16"),
+    "s1": ("sbuf", [P, QP], "bfloat16"),
+    "ys": ("sbuf", [P, QP], "bfloat16"),
+    "ps0": ("psum", [P, 512], "float32"),
+    "ps1": ("psum", [P, 512], "float32"),
+    "po": ("psum", [P, 512], "float32"),
+}
+SEMAPHORES = ["kvl", "ql", "arr", "sent", "zf", "ms0", "ms1", "rl0", "rl1", "mo", "cp", "st"]
+
+
+def _bits(m):
+    return [1 << i for i in range(m.bit_length()) if (m >> i) & 1]
+
+
+def _join(bs):
+    m = 0
+    for b in bs:
+        m |= b
+    return m
+
+
+def _shares(engines, n):
+    each = 1
+    while each * 2 * n <= len(engines):
+        each *= 2
+    return [engines[i * each:(i + 1) * each] for i in range(n)]
+
+
+def _plan(T, topo):
+    src = T.cores[T.tables["MEM"][0]]
+    others = [c for c in T.cores if c != src]
+    far = [c for c in others if topo.chip(c) != topo.chip(src)]
+    near = [c for c in others if topo.chip(c) == topo.chip(src)]
+    assert all(topo.may_write(src, c) for c in others)
+    calls = []
+    far_mask = 0
+    if far:
+        far_mask = topo.mask(src, far[0])
+        for c in far:
+            far_mask &= topo.mask(src, c)
+        calls.append(list(zip(far, _shares(_bits(far_mask), len(far)))))
+    if near:
+        near_mask = topo.mask(src, near[0]) & ~far_mask
+        calls.append(list(zip(near, _shares(_bits(near_mask), len(near)))))
+    return src, calls
+
+
+def rank_program(g, core, T, topo):
+    if T.rank_of(core) is None:
+        return
+    S = T.sem
+    src, calls = _plan(T, topo)
+    te, ve = g.tensor, g.vector
+
+    ve.memset(T.zero[:], 0.0).then_inc(S.zf, 1)
+
+    if core == src:
+        g.sync.dma_start(T.kv[:, 0:W], T.k[:]).then_inc(S.kvl, 16)
+        g.scalar.dma_start(T.kv[:, W:2 * W], T.v[:]).then_inc(S.kvl, 16)
+        g.sync.dma_start(T.qs[:], T.q[:]).then_inc(S.ql, 16)
+        g.wait_ge(S.kvl, 32)
+        left = 0
+        for call in calls:
+            trs = []
+            for dst, engines in call:
+                rid, pid, _ = topo.addr(dst)
+                trs.append(RemoteDMATransfer(dst_ids=[DstId(rid=rid, pnc=pid)], dma_engine_mask=_join(engines),
+                                             remote_sem=S.arr, src=T.kv[:], dst=T.kv[:]))
+                left += len(engines)
+            g.remote_dma_fused(trs, local_sem=S.sent)
+        g.wait_ge(S.sent, left)
+        te.wait_ge(S.kvl, 32)
+    else:
+        g.sync.dma_start(T.qs[:], T.q[:]).then_inc(S.ql, 16)
+        mine = [len(engines) for call in calls for dst, engines in call if dst == core]
+        te.wait_ge(S.arr, mine[0])
+    te.wait_ge(S.ql, 16)
+
+    for b in range(KB):
+        te.matmul(T["ps%d" % b][:, 0:QP], T.kv[:, b * P:(b + 1) * P], T.qs[:], start=True, stop=True) \
+            .then_inc(S["ms%d" % b], 1)
+    ve.wait_ge(S.zf, 1)
+    for b in range(KB):
+        ve.wait_ge(S["ms%d" % b], 1)
+        ve.tensor_tensor(T["s%d" % b][:], T["ps%d" % b][:, 0:QP], T.zero[:], AluOpType.max).then_inc(S["rl%d" % b], 1)
+    for b in range(KB):
+        te.wait_ge(S["rl%d" % b], 1)
+        mm = te.matmul(T.po[:, 0:QP], T.kv[:, W + b * P:W + (b + 1) * P], T["s%d" % b][:], start=(b == 0),
+                       stop=(b == KB - 1))
+    mm.then_inc(S.mo, 1)
+    ve.wait_ge(S.mo, 1)
+    ve.tensor_copy(T.ys[:], T.po[:, 0:QP]).then_inc(S.cp, 1)
+    g.sync.wait_ge(S.cp, 1)
+    g.sync.dma_start(T.y[:], T.ys[:]).then_inc(S.st, 16)
+    g.sync.wait_ge(S.st, 16)

@@ -5,19 +5,24 @@ P = 128
 QP = 256
 KB = 2
 W = KB * P
+NH = 2
+H = QP // NH
 
 SCRATCH = {
     "kv": ("sbuf", [P, 2 * W], "bfloat16"),
     "qs": ("sbuf", [P, QP], "bfloat16"),
-    "zero": ("sbuf", [P, QP], "float32"),
-    "s0": ("sbuf", [P, QP], "bfloat16"),
-    "s1": ("sbuf", [P, QP], "bfloat16"),
+    "zero": ("sbuf", [P, H], "float32"),
     "ys": ("sbuf", [P, QP], "bfloat16"),
-    "ps0": ("psum", [P, 512], "float32"),
-    "ps1": ("psum", [P, 512], "float32"),
-    "po": ("psum", [P, 512], "float32"),
 }
-SEMAPHORES = ["kvl", "ql", "arr", "sent", "zf", "ms0", "ms1", "rl0", "rl1", "mo", "cp", "st"]
+SEMAPHORES = ["kl", "vl", "ql", "arrk", "arrv", "sent", "zf", "cp", "st"]
+for _b in range(KB):
+    SCRATCH["s%d" % _b] = ("sbuf", [P, QP], "bfloat16")
+    for _h in range(NH):
+        SCRATCH["ps%d%d" % (_b, _h)] = ("psum", [P, 512], "float32")
+        SEMAPHORES += ["ms%d%d" % (_b, _h), "rl%d%d" % (_b, _h)]
+for _h in range(NH):
+    SCRATCH["po%d" % _h] = ("psum", [P, 512], "float32")
+    SEMAPHORES.append("mo%d" % _h)
 
 
 def _bits(m):
@@ -44,64 +49,77 @@ def _plan(T, topo):
     far = [c for c in others if topo.chip(c) != topo.chip(src)]
     near = [c for c in others if topo.chip(c) == topo.chip(src)]
     assert all(topo.may_write(src, c) for c in others)
-    calls = []
-    far_mask = 0
-    if far:
-        far_mask = topo.mask(src, far[0])
-        for c in far:
-            far_mask &= topo.mask(src, c)
-        calls.append(list(zip(far, _shares(_bits(far_mask), len(far)))))
-    if near:
-        near_mask = topo.mask(src, near[0]) & ~far_mask
-        calls.append(list(zip(near, _shares(_bits(near_mask), len(near)))))
-    return src, calls
+    far_mask = topo.mask(src, far[0])
+    for c in far:
+        far_mask &= topo.mask(src, c)
+    farp = list(zip(far, _shares(_bits(far_mask), len(far))))
+    near_mask = topo.mask(src, near[0]) & ~far_mask
+    nearp = list(zip(near, _shares(_bits(near_mask), len(near))))
+    return src, farp, nearp
 
 
 def rank_program(g, core, T, topo):
     if T.rank_of(core) is None:
         return
     S = T.sem
-    src, calls = _plan(T, topo)
+    src, farp, nearp = _plan(T, topo)
     te, ve = g.tensor, g.vector
 
     ve.memset(T.zero[:], 0.0).then_inc(S.zf, 1)
 
+    def send(plan, lo, hi, sem):
+        trs = []
+        n = 0
+        for dst, engines in plan:
+            rid, pid, _ = topo.addr(dst)
+            trs.append(RemoteDMATransfer(dst_ids=[DstId(rid=rid, pnc=pid)], dma_engine_mask=_join(engines),
+                                         remote_sem=sem, src=T.kv[:, lo:hi], dst=T.kv[:, lo:hi]))
+            n += len(engines)
+        g.remote_dma_fused(trs, local_sem=S.sent)
+        return n
+
     if core == src:
-        g.sync.dma_start(T.kv[:, 0:W], T.k[:]).then_inc(S.kvl, 16)
-        g.scalar.dma_start(T.kv[:, W:2 * W], T.v[:]).then_inc(S.kvl, 16)
+        g.sync.dma_start(T.kv[:, 0:W], T.k[:]).then_inc(S.kl, 16)
+        g.scalar.dma_start(T.kv[:, W:2 * W], T.v[:]).then_inc(S.vl, 16)
         g.sync.dma_start(T.qs[:], T.q[:]).then_inc(S.ql, 16)
-        g.wait_ge(S.kvl, 32)
-        left = 0
-        for call in calls:
-            trs = []
-            for dst, engines in call:
-                rid, pid, _ = topo.addr(dst)
-                trs.append(RemoteDMATransfer(dst_ids=[DstId(rid=rid, pnc=pid)], dma_engine_mask=_join(engines),
-                                             remote_sem=S.arr, src=T.kv[:], dst=T.kv[:]))
-                left += len(engines)
-            g.remote_dma_fused(trs, local_sem=S.sent)
+        g.wait_ge(S.kl, 16)
+        left = send(farp, 0, W, S.arrk)
+        g.wait_ge(S.vl, 16)
+        left += send(farp, W, 2 * W, S.arrv)
+        left += send(nearp, 0, 2 * W, S.arrk)
         g.wait_ge(S.sent, left)
-        te.wait_ge(S.kvl, 32)
+        kw, vw = (S.kl, 16), (S.vl, 16)
     else:
         g.sync.dma_start(T.qs[:], T.q[:]).then_inc(S.ql, 16)
-        mine = [len(engines) for call in calls for dst, engines in call if dst == core]
-        te.wait_ge(S.arr, mine[0])
-    te.wait_ge(S.ql, 16)
+        fm = [len(e) for d, e in farp if d == core]
+        nm = [len(e) for d, e in nearp if d == core]
+        if fm:
+            kw, vw = (S.arrk, fm[0]), (S.arrv, fm[0])
+        else:
+            kw, vw = (S.arrk, nm[0]), None
 
-    for b in range(KB):
-        te.matmul(T["ps%d" % b][:, 0:QP], T.kv[:, b * P:(b + 1) * P], T.qs[:], start=True, stop=True) \
-            .then_inc(S["ms%d" % b], 1)
+    te.wait_ge(S.ql, 16)
+    te.wait_ge(kw[0], kw[1])
+    for h in range(NH):
+        for b in range(KB):
+            te.matmul(T["ps%d%d" % (b, h)][:, 0:H], T.kv[:, b * P:(b + 1) * P], T.qs[:, h * H:(h + 1) * H],
+                      start=True, stop=True).then_inc(S["ms%d%d" % (b, h)], 1)
     ve.wait_ge(S.zf, 1)
-    for b in range(KB):
-        ve.wait_ge(S["ms%d" % b], 1)
-        ve.tensor_tensor(T["s%d" % b][:], T["ps%d" % b][:, 0:QP], T.zero[:], AluOpType.max).then_inc(S["rl%d" % b], 1)
-    for b in range(KB):
-        te.wait_ge(S["rl%d" % b], 1)
-        mm = te.matmul(T.po[:, 0:QP], T.kv[:, W + b * P:W + (b + 1) * P], T["s%d" % b][:], start=(b == 0),
-                       stop=(b == KB - 1))
-    mm.then_inc(S.mo, 1)
-    ve.wait_ge(S.mo, 1)
-    ve.tensor_copy(T.ys[:], T.po[:, 0:QP]).then_inc(S.cp, 1)
-    g.sync.wait_ge(S.cp, 1)
+    for h in range(NH):
+        for b in range(KB):
+            ve.wait_ge(S["ms%d%d" % (b, h)], 1)
+            ve.tensor_tensor(T["s%d" % b][:, h * H:(h + 1) * H], T["ps%d%d" % (b, h)][:, 0:H], T.zero[:],
+                             AluOpType.max).then_inc(S["rl%d%d" % (b, h)], 1)
+    if vw:
+        te.wait_ge(vw[0], vw[1])
+    for h in range(NH):
+        for b in range(KB):
+            te.wait_ge(S["rl%d%d" % (b, h)], 1)
+            mm = te.matmul(T["po%d" % h][:, 0:H], T.kv[:, W + b * P:W + (b + 1) * P], T["s%d" % b][:, h * H:(h + 1) * H],
+                           start=(b == 0), stop=(b == KB - 1))
+        mm.then_inc(S["mo%d" % h], 1)
+        ve.wait_ge(S["mo%d" % h], 1)
+        ve.tensor_copy(T.ys[:, h * H:(h + 1) * H], T["po%d" % h][:, 0:H]).then_inc(S.cp, 1)
+    g.sync.wait_ge(S.cp, NH)
     g.sync.dma_start(T.y[:], T.ys[:]).then_inc(S.st, 16)
     g.sync.wait_ge(S.st, 16)

from concourse.bass import DstId, RemoteDMATransfer
from concourse.mybir import AluOpType

P = 128
QP = 256
KB = 2
W = KB * P
NH = 2
H = QP // NH

SCRATCH = {
    "kv": ("sbuf", [P, 2 * W], "bfloat16"),
    "qs": ("sbuf", [P, QP], "bfloat16"),
    "zero": ("sbuf", [P, H], "float32"),
    "ys": ("sbuf", [P, QP], "bfloat16"),
}
SEMAPHORES = ["kl", "vl", "ql", "arrk", "arrv", "sent", "zf", "cp", "st"]
for _b in range(KB):
    SCRATCH["s%d" % _b] = ("sbuf", [P, QP], "bfloat16")
    for _h in range(NH):
        SCRATCH["ps%d%d" % (_b, _h)] = ("psum", [P, 512], "float32")
        SEMAPHORES += ["ms%d%d" % (_b, _h), "rl%d%d" % (_b, _h)]
for _h in range(NH):
    SCRATCH["po%d" % _h] = ("psum", [P, 512], "float32")
    SEMAPHORES.append("mo%d" % _h)


def _bits(m):
    return [1 << i for i in range(m.bit_length()) if (m >> i) & 1]


def _join(bs):
    m = 0
    for b in bs:
        m |= b
    return m


def _shares(engines, n):
    each = 1
    while each * 2 * n <= len(engines):
        each *= 2
    return [engines[i * each:(i + 1) * each] for i in range(n)]


def _plan(T, topo):
    src = T.cores[T.tables["MEM"][0]]
    others = [c for c in T.cores if c != src]
    far = [c for c in others if topo.chip(c) != topo.chip(src)]
    near = [c for c in others if topo.chip(c) == topo.chip(src)]
    assert all(topo.may_write(src, c) for c in others)
    far_mask = topo.mask(src, far[0])
    for c in far:
        far_mask &= topo.mask(src, c)
    farp = list(zip(far, _shares(_bits(far_mask), len(far))))
    near_mask = topo.mask(src, near[0]) & ~far_mask
    nearp = list(zip(near, _shares(_bits(near_mask), len(near))))
    return src, farp, nearp


def rank_program(g, core, T, topo):
    if T.rank_of(core) is None:
        return
    S = T.sem
    src, farp, nearp = _plan(T, topo)
    te, ve = g.tensor, g.vector

    ve.memset(T.zero[:], 0.0).then_inc(S.zf, 1)

    def send(plan, lo, hi, sem):
        trs = []
        n = 0
        for dst, engines in plan:
            rid, pid, _ = topo.addr(dst)
            trs.append(RemoteDMATransfer(dst_ids=[DstId(rid=rid, pnc=pid)], dma_engine_mask=_join(engines),
                                         remote_sem=sem, src=T.kv[:, lo:hi], dst=T.kv[:, lo:hi]))
            n += len(engines)
        g.remote_dma_fused(trs, local_sem=S.sent)
        return n

    if core == src:
        g.sync.dma_start(T.kv[:, 0:W], T.k[:]).then_inc(S.kl, 16)
        g.scalar.dma_start(T.kv[:, W:2 * W], T.v[:]).then_inc(S.vl, 16)
        g.sync.dma_start(T.qs[:], T.q[:]).then_inc(S.ql, 16)
        g.wait_ge(S.kl, 16)
        left = send(farp, 0, W, S.arrk)
        g.wait_ge(S.vl, 16)
        left += send(farp, W, 2 * W, S.arrv)
        left += send(nearp, 0, 2 * W, S.arrk)
        g.wait_ge(S.sent, left)
        kw, vw = (S.kl, 16), (S.vl, 16)
    else:
        g.sync.dma_start(T.qs[:], T.q[:]).then_inc(S.ql, 16)
        fm = [len(e) for d, e in farp if d == core]
        nm = [len(e) for d, e in nearp if d == core]
        if fm:
            kw, vw = (S.arrk, fm[0]), (S.arrv, fm[0])
        else:
            kw, vw = (S.arrk, nm[0]), None

    te.wait_ge(S.ql, 16)
    te.wait_ge(kw[0], kw[1])
    for h in range(NH):
        for b in range(KB):
            te.matmul(T["ps%d%d" % (b, h)][:, 0:H], T.kv[:, b * P:(b + 1) * P], T.qs[:, h * H:(h + 1) * H],
                      start=True, stop=True).then_inc(S["ms%d%d" % (b, h)], 1)
    ve.wait_ge(S.zf, 1)
    for h in range(NH):
        for b in range(KB):
            ve.wait_ge(S["ms%d%d" % (b, h)], 1)
            ve.tensor_tensor(T["s%d" % b][:, h * H:(h + 1) * H], T["ps%d%d" % (b, h)][:, 0:H], T.zero[:],
                             AluOpType.max).then_inc(S["rl%d%d" % (b, h)], 1)
    if vw:
        te.wait_ge(vw[0], vw[1])
    for h in range(NH):
        for b in range(KB):
            te.wait_ge(S["rl%d%d" % (b, h)], 1)
            mm = te.matmul(T["po%d" % h][:, 0:H], T.kv[:, W + b * P:W + (b + 1) * P], T["s%d" % b][:, h * H:(h + 1) * H],
                           start=(b == 0), stop=(b == KB - 1))
        mm.then_inc(S["mo%d" % h], 1)
        ve.wait_ge(S["mo%d" % h], 1)
        ve.tensor_copy(T.ys[:, h * H:(h + 1) * H], T["po%d" % h][:, 0:H]).then_inc(S.cp, 1)
    g.sync.wait_ge(S.cp, NH)
    g.sync.dma_start(T.y[:], T.ys[:]).then_inc(S.st, 16)
    g.sync.wait_ge(S.st, 16)
